import numpy as np
import ml_dtypes


def mxq(x, axis, fmt="e4m3"):
    dtype, down = {"e4m3": (ml_dtypes.float8_e4m3fn, 7), "e5m2": (ml_dtypes.float8_e5m2, 14)}[fmt]
    v = np.moveaxis(np.asarray(x, np.float32).astype(ml_dtypes.bfloat16).astype(np.float64), axis, -1)
    blocks = v.reshape(v.shape[:-1] + (-1, 32))
    amax = np.abs(blocks).max(-1, keepdims=True)
    byte = np.maximum(np.where(amax > 0, np.frexp(amax)[1] - 1 + 127, 0) - down, 1)
    scale = np.exp2(byte - 127.0)
    codes = (blocks / scale).astype(np.float32).astype(dtype).astype(np.float64)
    return np.moveaxis((codes * scale).reshape(v.shape), -1, axis)


WIDE = False


def mx_kscale(k):
    if not WIDE:
        return np.ones(k)
    levels = np.array([10, -10, 5, -5, 0])
    if k % 512:
        return np.exp2(np.random.permutation(np.resize(levels, k // 32))).repeat(32)
    a = np.empty((k // 512, 16))
    for p in range(k // 512):
        a[p, :8] = np.random.permutation(np.resize(levels, 8))
        for g in range(8):
            far = levels[np.abs(levels - a[p, g]) >= 10]
            a[p, g + 8] = far[np.random.randint(len(far))]
    return np.exp2(a.ravel()).repeat(32)


def f64(x):
    return np.asarray(x).astype(np.float64)


def striped(idx):
    return np.tile(idx.reshape(-1, 16).T, (8, 1)).astype(np.uint16)


def unstriped(offs):
    return offs[:16].T.reshape(-1).astype(np.int64)


def striped8(idx):
    return np.concatenate([x.reshape(-1, 16).T for x in idx]).astype(np.uint16)


def runs(offs, k):
    lists = np.stack([offs[16 * r : 16 * r + 16].T.reshape(-1) for r in range(8)]).astype(np.int64)
    return lists[np.arange(k) % 512 // 64]


def pack_weight(w):
    k, n = w.shape
    w = f64(np.asarray(w, np.float32).astype(ml_dtypes.bfloat16)).reshape(k // 32, 32, n)
    amax = np.abs(w).max(1)
    byte = np.clip(np.where(amax > 0, np.frexp(amax)[1] - 1 + 127 - 7, 1), 1, 254)
    scaled = (w * np.exp2(127.0 - byte)[:, None, :]).reshape(k, n).astype(np.float32)
    words = np.ascontiguousarray(scaled.reshape(k // 512, 128, 4, n).transpose(0, 1, 3, 2)).astype(ml_dtypes.float8_e4m3fn).view(np.uint8)
    return words, np.ascontiguousarray(byte.astype(np.uint8).reshape(k // 512, 16, n))


def unpack_weight(words, scales):
    g, p, n, _ = words.shape
    vals = np.ascontiguousarray(words).view(ml_dtypes.float8_e4m3fn).astype(np.float64) * np.repeat(np.exp2(scales.astype(np.float64) - 127.0), 8, axis=1)[..., None]
    return vals.transpose(0, 1, 3, 2).reshape(g * 512, n)


def sigmoid(v):
    return 1.0 / (1.0 + np.exp(-np.maximum(v, -700.0)))

def planes(y):
    n, m = y.shape
    v = y.astype(np.float32).astype(ml_dtypes.bfloat16).astype(np.float64).reshape(n // 32, 32, m)
    top = np.abs(v).max(1)
    byte = np.clip(np.where(top > 0, np.frexp(top)[1] - 1 + 127 - 7, 1), 1, 254)
    codes = (v * np.exp2(127.0 - byte)[:, None, :]).reshape(n, m).astype(np.float32).astype(ml_dtypes.float8_e4m3fn).view(np.uint8)
    words = codes.reshape(n // 512, 128, 4, m).transpose(0, 1, 3, 2)
    return np.ascontiguousarray(words), np.ascontiguousarray(byte.astype(np.uint8).reshape(n // 512, 16, m))


K, T, S, V, H, W, U = 512, 2048, 512, 256, 512, 1024, 1024


def setup_inputs():
    n = np.random.standard_normal
    s = mx_kscale(K)[:, None]
    u = mx_kscale(S)
    packed_xT = pack_weight(n((K, T)) * s)
    packed_w1 = pack_weight(n((K, H)) / np.sqrt(K) / s)
    packed_w2 = pack_weight(n((K, H)) / np.sqrt(K) / s)
    return {
        "x_words": packed_xT[0],
        "x_scales": packed_xT[1],
        "w1_words": packed_w1[0],
        "w1_scales": packed_w1[1],
        "w2_words": packed_w2[0],
        "w2_scales": packed_w2[1],
        "ga": (np.random.uniform(0.5, 1.5, (H, 1)) * u[:, None]).astype(np.float32),
        "gb": (np.random.uniform(0.5, 1.5, (H, 1)) / u[:, None]).astype(np.float32),
        "mem": n((S, U)).astype(np.float32),
        "offs": striped(np.random.permutation(T)[:S]),
        "two": striped(np.random.permutation(T)[:V]),
        "n1": striped(np.random.randint(0, S, W)),
        "n2": striped8(np.stack([np.random.permutation(V) for _ in range(8)])),
        "n3": striped8(np.stack([np.random.permutation(V) for _ in range(8)])),
        "n4": striped(np.random.permutation(U)[:V]),
    }


def reference(x_words, x_scales, w1_words, w1_scales, w2_words, w2_scales, ga, gb, mem, offs, two, n1, n2, n3, n4):
    xq = unpack_weight(x_words, x_scales)[:, unstriped(offs)]
    a = unpack_weight(w1_words, w1_scales).T @ xq
    mb = a[:, unstriped(n1)]
    mn = mb.reshape(H, S, 2).min(axis=2)
    mx = mb.reshape(H, S, 2).max(axis=2)
    z = f64(ga) * ((a - mn) * sigmoid(mx))
    x_two = unpack_weight(x_words, x_scales)[:, unstriped(two)]
    b = unpack_weight(w2_words, w2_scales).T @ x_two
    pa = b[np.arange(H)[:, None], runs(n2, H)]
    pb = b[np.arange(H)[:, None], runs(n3, H)]
    z2 = f64(gb) * (np.maximum(np.maximum(b, pa), pb) - (0.5 * (np.minimum(np.minimum(b, pa), pb))))
    s = 0.0625 * ((mxq(z, 0, "e4m3").T @ mxq(z2, 0, "e4m3")))
    out = f64(mem).copy()
    out[:, unstriped(n4)] = s
    return (out,) + planes(out)

@@ -1,0 +1,239 @@
+from contextlib import ExitStack
+
+import concourse.mybir as mybir
+
+F32 = mybir.dt.float32
+BF16 = mybir.dt.bfloat16
+I32 = mybir.dt.int32
+U32 = mybir.dt.uint32
+U16 = mybir.dt.uint16
+U8 = mybir.dt.uint8
+FP8X4 = mybir.dt.float8_e4m3fn_x4
+ALU = mybir.AluOpType
+ACT = mybir.ActivationFunctionType
+
+P = 128
+T, S, V, H, U = 2048, 512, 256, 512, 1024
+FLOPS = 2 * 512 * H * S + 2 * 512 * H * V + 2 * H * S * V
+
+
+def as_words(packed):
+    return packed[0].rearrange("p n t -> p (n t)").bitcast(I32)
+
+
+def tile_picked_kqghardrangepage_none_po_kernel(tc, x_words, x_scales, w1_words, w1_scales, w2_words, w2_scales, ga, gb, mem, offs, two, n1, n2, n3, n4, out_0, out_1, out_2):
+    nc = tc.nc
+    with ExitStack() as ctx:
+        sb = ctx.enter_context(tc.tile_pool(name="sb", bufs=1))
+        ps = ctx.enter_context(tc.psum_pool(name="ps", bufs=1))
+
+        def new(name, shape, dtype, tag=None):
+            return sb.tile(shape, dtype, name=name, tag=tag or name, align_bytes=64)
+
+        def load_list(name, src):
+            t = sb.tile(list(src.shape), U16, name=name)
+            nc.sync.dma_start(t[:], src)
+            return t
+
+        def load_scales(queues, plane, src):
+            for q in range(4):
+                queues[q].dma_start(plane[32 * q : 32 * q + 4, :].bitcast(I32), src[0, 4 * q : 4 * q + 4, :].bitcast(I32))
+
+        xs = new("xs", [P, T], U8, "slot0")
+        w2s_raw = new("w2s_raw", [P, H], U8, "slot3")
+        w1s_raw = new("w1s_raw", [P, H], U8, "hi0")
+        nc.vector.memset(xs[:, : T // 2].bitcast(I32), 0)
+        nc.gpsimd.memset(xs[:, T // 2 :].bitcast(I32), 0)
+        for plane in (w2s_raw, w1s_raw):
+            nc.gpsimd.memset(plane[:].bitcast(I32), 0)
+
+        two_l = load_list("two_l", two)
+        offs_l = load_list("offs_l", offs)
+        load_scales([nc.sync] * 4, xs, x_scales)
+        xw = new("xw", [P, T], I32, "slot2")
+        nc.sync.dma_start(xw[:], as_words(x_words))
+        w2_raw = new("w2_raw", [P, H], I32, "slot1")
+        nc.sync.dma_start(w2_raw[:], as_words(w2_words))
+        load_scales([nc.sync] * 4, w2s_raw, w2_scales)
+        n2_l = load_list("n2_l", n2)
+        n3_l = load_list("n3_l", n3)
+        w1_raw = new("w1_raw", [P, H], I32, "lo0")
+        nc.sync.dma_start(w1_raw[:], as_words(w1_words))
+        load_scales([nc.sync] * 4, w1s_raw, w1_scales)
+        n1_l = load_list("n1_l", n1)
+        bw = [new(f"bw{t}", [P, 2 * V], F32) for t in range(4)]
+        aw = [new(f"aw{t}", [P, S + 16], F32) for t in range(4)]
+        for t in range(4):
+            nc.gpsimd.memset(bw[t][:, V:], 0.0)
+        for t in range(4):
+            nc.gpsimd.memset(aw[t][:, S:], 0.0)
+        gb_t = new("gb_t", [P, 4], F32)
+        nc.sync.dma_start(gb_t[:], gb.rearrange("(p t) o -> p (t o)", t=4))
+        ga_t = new("ga_t", [P, 4], F32)
+        nc.sync.dma_start(ga_t[:], ga.rearrange("(p t) o -> p (t o)", t=4))
+        n4_l = load_list("n4_l", n4)
+        mem_rows = mem.rearrange("(p t) u -> p t u", t=4)
+        out_rows = out_0.rearrange("(p t) u -> p t u", t=4)
+
+        def deal(dst, src):
+            nc.vector.tensor_copy(dst[:].rearrange("p (t m) -> p m t", t=4), src[:].rearrange("p (m t) -> p m t", t=4))
+
+        xb_s = new("xb_s", [P, V], U8)
+        nc.vector.tensor_copy(xb_s[:], xs[:].indirect(two_l[:]))
+        xa_s = new("xa_s", [P, S], U8)
+        nc.vector.tensor_copy(xa_s[:], xs[:].indirect(offs_l[:]))
+        w2s = new("w2s", [P, H], U8)
+        deal(w2s, w2s_raw)
+        xb = new("xb", [P, V], U32)
+        nc.vector.tensor_copy(xb[:], xw[:].bitcast(U32).indirect(two_l[:]))
+        w2 = new("w2", [P, H], I32)
+        deal(w2, w2_raw)
+
+        def product(out, lhs, lhs_s, t, rhs, rhs_s):
+            cols = slice(P * t, P * (t + 1))
+            nc.tensor.matmul_mx(out=out, lhsT=lhs[:, cols].bitcast(FP8X4), lhsT_scale=lhs_s[:, cols], rhs=rhs[:].bitcast(FP8X4), rhs_scale=rhs_s[:], start=True, stop=True)
+
+        b_ps = [ps.tile([P, 2, V], F32, name=f"b_ps{h}") for h in range(2)]
+        for t in range(4):
+            product(b_ps[t // 2][:, t % 2, :], w2, w2s, t, xb, xb_s)
+
+        xa = new("xa", [P, S], U32, "hi1")
+        nc.vector.tensor_copy(xa[:], xw[:].bitcast(U32).indirect(offs_l[:]))
+        w1s = new("w1s", [P, H], U8)
+        deal(w1s, w1s_raw)
+        w1 = new("w1", [P, H], I32, "lo1")
+        deal(w1, w1_raw)
+        a_ps = [ps.tile([P, S], F32, name=f"a_ps{t}") for t in range(4)]
+        for t in range(4):
+            product(a_ps[t][:], w1, w1s, t, xa, xa_s)
+
+        page = [new(f"page{t}", [P, U], F32, f"slot{t}") for t in range(4)]
+        for t in range(4):
+            nc.sync.dma_start(page[t][:], mem_rows[:, t, :])
+
+        pa = [new(f"pa{h}", [P, 2, V], F32) for h in range(2)]
+        pb = [new(f"pb{h}", [P, 2, V], F32) for h in range(2)]
+        for t in range(4):
+            nc.scalar.copy(bw[t][:, :V], b_ps[t // 2][:, t % 2, :])
+            nc.scalar.activation(pa[t // 2][:, t % 2, :], bw[t][:].indirect(n2_l[:]), ACT.Copy)
+            nc.scalar.activation(pb[t // 2][:, t % 2, :], bw[t][:].indirect(n3_l[:]), ACT.Copy)
+        for t in range(2):
+            nc.vector.tensor_copy(aw[t][:, :S], a_ps[t][:])
+
+        u = new("u", [P, 4, V], F32)
+        for h in range(2):
+            hi = new(f"hi{h}", [P, 2, V], F32)
+            lo = new(f"lo{h}", [P, 2, V], F32)
+            top = new(f"top{h}", [P, 2, V], F32)
+            low = new(f"low{h}", [P, 2, V], F32)
+            nc.vector.tensor_tensor(hi[:], pa[h][:], pb[h][:], ALU.max)
+            nc.vector.tensor_tensor(lo[:], pa[h][:], pb[h][:], ALU.min)
+            nc.vector.tensor_tensor(top[:], hi[:], b_ps[h][:], ALU.max)
+            nc.vector.tensor_tensor(low[:], lo[:], b_ps[h][:], ALU.min)
+            nc.vector.scalar_tensor_tensor(u[:, 2 * h : 2 * h + 2, :], low[:], -0.5, top[:], ALU.mult, ALU.add)
+
+        mx, mn, sg, df, mb = {}, {}, {}, {}, {}
+        zb = new("zb", [P, 4, S], BF16)
+        zg = new("zg", [P, S, 4], BF16)
+        z2g = new("z2g", [P, V, 4], BF16)
+        z2q = new("z2q", [P, V], U32)
+        z2s = new("z2s", [P, V], U8)
+        pieces = [(0, 0, S), (1, 0, S), (2, 0, S), (3, 0, S // 2), (3, S // 2, S)]
+
+        def fetch(i):
+            t, lo_col, hi_col = pieces[i]
+            if t >= 2 and lo_col == 0:
+                nc.scalar.copy(aw[t][:, :S], a_ps[t][:])
+            mb[i] = new(f"mb{i}", [P, 2 * (hi_col - lo_col)], F32, f"mx{i - 2}" if i >= 2 else None)
+            for c in range(lo_col, hi_col, S // 2):
+                nc.scalar.activation(mb[i][:, 2 * (c - lo_col) : 2 * (c - lo_col) + S], aw[t][:].indirect(n1_l[:, c // 8 : c // 8 + 32]), ACT.Copy)
+
+        def larger(i):
+            t, lo_col, hi_col = pieces[i]
+            pairs = mb[i][:].rearrange("p (j e) -> p j e", e=2)
+            mx[i] = new(f"mx{i}", [P, hi_col - lo_col], F32)
+            nc.vector.tensor_tensor(mx[i][:], pairs[:, :, 0], pairs[:, :, 1], ALU.max)
+            sg[i] = new(f"sg{i}", [P, hi_col - lo_col], F32)
+            nc.scalar.activation(sg[i][:], mx[i][:], ACT.Sigmoid)
+
+        def smaller(i):
+            t, lo_col, hi_col = pieces[i]
+            pairs = mb[i][:].rearrange("p (j e) -> p j e", e=2)
+            mn[i] = new(f"mn{i}", [P, hi_col - lo_col], F32)
+            nc.vector.tensor_tensor(mn[i][:], pairs[:, :, 0], pairs[:, :, 1], ALU.min)
+
+        def differ(i):
+            t, lo_col, hi_col = pieces[i]
+            df[i] = new(f"df{i}", [P, hi_col - lo_col], F32)
+            nc.vector.tensor_tensor(df[i][:], aw[t][:, lo_col:hi_col], mn[i][:], ALU.subtract)
+
+        def gate(i):
+            t, lo_col, hi_col = pieces[i]
+            nc.vector.scalar_tensor_tensor(
+                zb[:, t, :].rearrange("p (s m) -> p m s", s=4)[:, lo_col // 4 : hi_col // 4, :],
+                df[i][:].rearrange("p (m s) -> p m s", s=4),
+                ga_t[:, t : t + 1],
+                sg[i][:].rearrange("p (m s) -> p m s", s=4),
+                ALU.mult,
+                ALU.mult,
+            )
+
+        def weave(copy, h):
+            copy(
+                zg[:].rearrange("p (s h c i) t -> p h s c t i", s=4, h=2, i=4)[:, h],
+                zb[:].rearrange("p t (s h c i) -> p h s c t i", s=4, h=2, i=4)[:, h],
+            )
+
+        fetch(0)
+        fetch(1)
+        larger(0)
+        nc.vector.tensor_tensor(
+            z2g[:].rearrange("p (c i) t -> p c t i", i=4),
+            u[:].rearrange("p t (c i) -> p c t i", i=4),
+            gb_t[:].unsqueeze(1).unsqueeze(3).broadcast_to([P, V // 4, 4, 4]),
+            ALU.mult,
+        )
+        smaller(0)
+        nc.vector.quantize_mx(out=z2q[:].bitcast(FP8X4), scales=z2s[:], in_=z2g[:].rearrange("p c t -> p (c t)"))
+        for i in range(1, len(pieces)):
+            if i + 1 < len(pieces):
+                fetch(i + 1)
+            larger(i)
+            differ(i - 1)
+            smaller(i)
+            if i > 1:
+                gate(i - 2)
+        differ(4)
+        gate(3)
+        weave(nc.scalar.copy, 0)
+        gate(4)
+        weave(nc.vector.tensor_copy, 1)
+        zq = new("zq", [P, S], U32)
+        zs = new("zs", [P, S], U8)
+        nc.vector.quantize_mx(out=zq[:].bitcast(FP8X4), scales=zs[:], in_=zg[:].rearrange("p c t -> p (c t)"))
+
+        s_ps = [ps.tile([P, 2, V], F32, name=f"s_ps{h}") for h in range(2)]
+        s_sb = [new(f"s_sb{t}", [P, V], F32) for t in range(4)]
+        for t in range(4):
+            product(s_ps[t % 2][:, t // 2, :], zq, zs, t, z2q, z2s)
+        for t in range(4):
+            nc.vector.tensor_scalar(s_sb[t][:], s_ps[t % 2][:, t // 2, :], 0.0625, None, ALU.mult)
+
+        grouped = new("grouped", [P, U, 4], BF16)
+        words = new("words", [P, U], I32)
+        scales = new("scales", [P, U], U8)
+        half = U // 2
+        for t in range(4):
+            nc.scalar.activation(page[t][:].indirect(n4_l[:]), s_sb[t][:], ACT.Copy)
+            nc.sync.dma_start(out_rows[:, t, :], page[t][:])
+            if t < 3:
+                nc.vector.tensor_copy(grouped[:, :, t], page[t][:])
+        out_words = as_words(out_1)
+        for h in range(2):
+            cols = slice(half * h, half * (h + 1))
+            nc.vector.tensor_copy(grouped[:, cols, 3], page[3][:, cols])
+            nc.vector.quantize_mx(out=words[:, cols].bitcast(FP8X4), scales=scales[:, cols], in_=grouped[:, cols, :].rearrange("p c t -> p (c t)"))
+            nc.sync.dma_start(out_words[:, cols], words[:, cols])
+        for q in range(4):
+            queue = nc.scalar if q % 2 else nc.sync
+            queue.dma_start(out_2[0, 4 * q : 4 * q + 4, :].bitcast(I32), scales[32 * q : 32 * q + 4, :].bitcast(I32))

@@ -41,28 +41,31 @@ def tile_picked_kqghardrangepage_none_po_kernel(tc, x_words, x_scales, w1_words,
 
         xs = new("xs", [P, T], U8, "slot0")
         w2s_raw = new("w2s_raw", [P, H], U8, "slot3")
-        w1s_raw = new("w1s_raw", [P, H], U8, "hi0")
+        w1s_raw = new("w1s_raw", [P, H], U8, "ends")
         nc.vector.memset(xs[:, : T // 2].bitcast(I32), 0)
         nc.gpsimd.memset(xs[:, T // 2 :].bitcast(I32), 0)
         for plane in (w2s_raw, w1s_raw):
             nc.gpsimd.memset(plane[:].bitcast(I32), 0)
+        warm = new("warm", [P, 2], F32)
+        nc.vector.memset(warm[:, 0:1], 0.0)
 
+        nc.scalar.activation(warm[:, 1:2], warm[:, 0:1], ACT.Sigmoid)
         two_l = load_list("two_l", two)
         offs_l = load_list("offs_l", offs)
+        w2_raw = new("w2_raw", [P, H], I32, "slot1")
+        nc.sync.dma_start(w2_raw[:], as_words(w2_words))
         load_scales([nc.sync] * 4, xs, x_scales)
         xw = new("xw", [P, T], I32, "slot2")
         nc.sync.dma_start(xw[:], as_words(x_words))
-        w2_raw = new("w2_raw", [P, H], I32, "slot1")
-        nc.sync.dma_start(w2_raw[:], as_words(w2_words))
         load_scales([nc.sync] * 4, w2s_raw, w2_scales)
         n2_l = load_list("n2_l", n2)
         n3_l = load_list("n3_l", n3)
-        w1_raw = new("w1_raw", [P, H], I32, "lo0")
+        w1_raw = new("w1_raw", [P, H], I32)
         nc.sync.dma_start(w1_raw[:], as_words(w1_words))
         load_scales([nc.sync] * 4, w1s_raw, w1_scales)
         n1_l = load_list("n1_l", n1)
         bw = [new(f"bw{t}", [P, 2 * V], F32) for t in range(4)]
-        aw = [new(f"aw{t}", [P, S + 16], F32) for t in range(4)]
+        aw = [new(f"aw{t}", [P, (2 * S if t < 3 else S) + 16], F32) for t in range(4)]
         for t in range(4):
             nc.gpsimd.memset(bw[t][:, V:], 0.0)
         for t in range(4):
@@ -78,34 +81,40 @@ def tile_picked_kqghardrangepage_none_po_kernel(tc, x_words, x_scales, w1_words,
         def deal(dst, src):
             nc.vector.tensor_copy(dst[:].rearrange("p (t m) -> p m t", t=4), src[:].rearrange("p (m t) -> p m t", t=4))
 
+        def deal_bytes(dst, src):
+            nc.vector.tensor_copy(dst[:].rearrange("p (t m) -> p t m", t=4), src[:].rearrange("p (m t) -> p t m", t=4))
+
+        w2 = new("w2", [P, H], I32)
+        deal(w2, w2_raw)
         xb_s = new("xb_s", [P, V], U8)
         nc.vector.tensor_copy(xb_s[:], xs[:].indirect(two_l[:]))
         xa_s = new("xa_s", [P, S], U8)
         nc.vector.tensor_copy(xa_s[:], xs[:].indirect(offs_l[:]))
-        w2s = new("w2s", [P, H], U8)
-        deal(w2s, w2s_raw)
         xb = new("xb", [P, V], U32)
         nc.vector.tensor_copy(xb[:], xw[:].bitcast(U32).indirect(two_l[:]))
-        w2 = new("w2", [P, H], I32)
-        deal(w2, w2_raw)
+        w2s = new("w2s", [P, H], U8)
+        deal_bytes(w2s, w2s_raw)
 
-        def product(out, lhs, lhs_s, t, rhs, rhs_s):
-            cols = slice(P * t, P * (t + 1))
-            nc.tensor.matmul_mx(out=out, lhsT=lhs[:, cols].bitcast(FP8X4), lhsT_scale=lhs_s[:, cols], rhs=rhs[:].bitcast(FP8X4), rhs_scale=rhs_s[:], start=True, stop=True)
+        def block(tile_, t):
+            return tile_[:, P * t : P * (t + 1)]
+
+        def product(out, lhs, lhs_s, rhs, rhs_s):
+            nc.tensor.matmul_mx(out=out, lhsT=lhs.bitcast(FP8X4), lhsT_scale=lhs_s, rhs=rhs[:].bitcast(FP8X4), rhs_scale=rhs_s[:], start=True, stop=True)
 
         b_ps = [ps.tile([P, 2, V], F32, name=f"b_ps{h}") for h in range(2)]
         for t in range(4):
-            product(b_ps[t // 2][:, t % 2, :], w2, w2s, t, xb, xb_s)
+            product(b_ps[t // 2][:, t % 2, :], block(w2, t), block(w2s, t), xb, xb_s)
 
-        xa = new("xa", [P, S], U32, "hi1")
+        xa = new("xa", [P, S], U32)
         nc.vector.tensor_copy(xa[:], xw[:].bitcast(U32).indirect(offs_l[:]))
         w1s = new("w1s", [P, H], U8)
-        deal(w1s, w1s_raw)
-        w1 = new("w1", [P, H], I32, "lo1")
-        deal(w1, w1_raw)
-        a_ps = [ps.tile([P, S], F32, name=f"a_ps{t}") for t in range(4)]
-        for t in range(4):
-            product(a_ps[t][:], w1, w1s, t, xa, xa_s)
+        deal_bytes(w1s, w1s_raw)
+        w1 = [new("w1_first", [P, H // 2], I32, "ends"), new("w1_second", [P, H // 2], I32)]
+        for h in range(2):
+            nc.vector.tensor_copy(w1[h][:].rearrange("p (t m) -> p m t", t=2), w1_raw[:].rearrange("p (m t) -> p m t", t=4)[:, :, 2 * h : 2 * h + 2])
+        a_ps = [ps.tile([P, S], F32, name=f"a_ps{t}") for t in range(2)]
+        for t in range(2):
+            product(a_ps[t][:], block(w1[0], t), block(w1s, t), xa, xa_s)
 
         page = [new(f"page{t}", [P, U], F32, f"slot{t}") for t in range(4)]
         for t in range(4):
@@ -121,16 +130,29 @@ def tile_picked_kqghardrangepage_none_po_kernel(tc, x_words, x_scales, w1_words,
             nc.vector.tensor_copy(aw[t][:, :S], a_ps[t][:])
 
         u = new("u", [P, 4, V], F32)
-        for h in range(2):
-            hi = new(f"hi{h}", [P, 2, V], F32)
-            lo = new(f"lo{h}", [P, 2, V], F32)
-            top = new(f"top{h}", [P, 2, V], F32)
-            low = new(f"low{h}", [P, 2, V], F32)
-            nc.vector.tensor_tensor(hi[:], pa[h][:], pb[h][:], ALU.max)
-            nc.vector.tensor_tensor(lo[:], pa[h][:], pb[h][:], ALU.min)
-            nc.vector.tensor_tensor(top[:], hi[:], b_ps[h][:], ALU.max)
-            nc.vector.tensor_tensor(low[:], lo[:], b_ps[h][:], ALU.min)
-            nc.vector.scalar_tensor_tensor(u[:, 2 * h : 2 * h + 2, :], low[:], -0.5, top[:], ALU.mult, ALU.add)
+        z2b = new("z2b", [P, 4, V], BF16, "mx1")
+        top, low = {}, {}
+
+        def of_two(h):
+            ends = new(f"ends{h}", [P, 2, 2, V], F32, "ends")
+            nc.vector.tensor_tensor(ends[:, 0], pa[h][:], pb[h][:], ALU.min)
+            nc.vector.tensor_tensor(ends[:, 1], pa[h][:], pb[h][:], ALU.max)
+            return ends
+
+        def of_three(h, ends):
+            low[h] = new(f"low{h}", [P, 2, V], F32, "mn" if h else None)
+            top[h] = new(f"top{h}", [P, 2, V], F32)
+            nc.vector.tensor_tensor(low[h][:], ends[:, 0], b_ps[h][:], ALU.min)
+            nc.vector.tensor_tensor(top[h][:], ends[:, 1], b_ps[h][:], ALU.max)
+            a_ps.append(ps.tile([P, S], F32, name=f"a_ps{2 + h}", tag=f"b_ps{h}"))
+            product(a_ps[2 + h][:], block(w1[1], h), block(w1s, 2 + h), xa, xa_s)
+
+        def spread(h):
+            nc.vector.scalar_tensor_tensor(u[:, 2 * h : 2 * h + 2, :], low[h][:], -0.5, top[h][:], ALU.mult, ALU.add)
+
+        def weigh(h):
+            for t in (2 * h, 2 * h + 1):
+                nc.vector.tensor_scalar(z2b[:, t, :], u[:, t, :], gb_t[:, t : t + 1], None, ALU.mult)
 
         mx, mn, sg, df, mb = {}, {}, {}, {}, {}
         zb = new("zb", [P, 4, S], BF16)
@@ -140,18 +162,19 @@ def tile_picked_kqghardrangepage_none_po_kernel(tc, x_words, x_scales, w1_words,
         z2s = new("z2s", [P, V], U8)
         pieces = [(0, 0, S), (1, 0, S), (2, 0, S), (3, 0, S // 2), (3, S // 2, S)]
 
+        larger_slot = ["ends", "mx1", "df0", "df1", "df2"]
+
         def fetch(i):
             t, lo_col, hi_col = pieces[i]
             if t >= 2 and lo_col == 0:
                 nc.scalar.copy(aw[t][:, :S], a_ps[t][:])
-            mb[i] = new(f"mb{i}", [P, 2 * (hi_col - lo_col)], F32, f"mx{i - 2}" if i >= 2 else None)
-            for c in range(lo_col, hi_col, S // 2):
-                nc.scalar.activation(mb[i][:, 2 * (c - lo_col) : 2 * (c - lo_col) + S], aw[t][:].indirect(n1_l[:, c // 8 : c // 8 + 32]), ACT.Copy)
+            mb[i] = new(f"mb{i}", [P, 2 * (hi_col - lo_col)], F32, larger_slot[i - 2] if i >= 2 else None)
+            nc.scalar.activation(mb[i][:], aw[t][:].indirect(n1_l[:, lo_col // 8 : hi_col // 8]), ACT.Copy)
 
         def larger(i):
             t, lo_col, hi_col = pieces[i]
             pairs = mb[i][:].rearrange("p (j e) -> p j e", e=2)
-            mx[i] = new(f"mx{i}", [P, hi_col - lo_col], F32)
+            mx[i] = new(f"mx{i}", [P, hi_col - lo_col], F32, larger_slot[i])
             nc.vector.tensor_tensor(mx[i][:], pairs[:, :, 0], pairs[:, :, 1], ALU.max)
             sg[i] = new(f"sg{i}", [P, hi_col - lo_col], F32)
             nc.scalar.activation(sg[i][:], mx[i][:], ACT.Sigmoid)
@@ -159,7 +182,7 @@ def tile_picked_kqghardrangepage_none_po_kernel(tc, x_words, x_scales, w1_words,
         def smaller(i):
             t, lo_col, hi_col = pieces[i]
             pairs = mb[i][:].rearrange("p (j e) -> p j e", e=2)
-            mn[i] = new(f"mn{i}", [P, hi_col - lo_col], F32)
+            mn[i] = new(f"mn{i}", [P, hi_col - lo_col], F32, "mn")
             nc.vector.tensor_tensor(mn[i][:], pairs[:, :, 0], pairs[:, :, 1], ALU.min)
 
         def differ(i):
@@ -170,54 +193,59 @@ def tile_picked_kqghardrangepage_none_po_kernel(tc, x_words, x_scales, w1_words,
         def gate(i):
             t, lo_col, hi_col = pieces[i]
             nc.vector.scalar_tensor_tensor(
-                zb[:, t, :].rearrange("p (s m) -> p m s", s=4)[:, lo_col // 4 : hi_col // 4, :],
-                df[i][:].rearrange("p (m s) -> p m s", s=4),
+                zb[:, t, lo_col:hi_col],
+                df[i][:],
                 ga_t[:, t : t + 1],
-                sg[i][:].rearrange("p (m s) -> p m s", s=4),
+                sg[i][:],
                 ALU.mult,
                 ALU.mult,
             )
 
         def weave(copy, h):
             copy(
-                zg[:].rearrange("p (s h c i) t -> p h s c t i", s=4, h=2, i=4)[:, h],
-                zb[:].rearrange("p t (s h c i) -> p h s c t i", s=4, h=2, i=4)[:, h],
+                zg[:].rearrange("p (s h m) t -> p h s m t", s=4, h=2)[:, h],
+                zb[:].rearrange("p t (h m s) -> p h s m t", s=4, h=2)[:, h],
             )
 
+        of_three(0, of_two(0))
+        spread(0)
+        ends = of_two(1)
+        weigh(0)
+        of_three(1, ends)
         fetch(0)
         fetch(1)
         larger(0)
-        nc.vector.tensor_tensor(
-            z2g[:].rearrange("p (c i) t -> p c t i", i=4),
-            u[:].rearrange("p t (c i) -> p c t i", i=4),
-            gb_t[:].unsqueeze(1).unsqueeze(3).broadcast_to([P, V // 4, 4, 4]),
-            ALU.mult,
-        )
+        spread(1)
         smaller(0)
+        weigh(1)
+        differ(0)
+        nc.vector.tensor_copy(z2g[:], z2b[:].rearrange("p t v -> p v t"))
+        fetch(2)
+        larger(1)
         nc.vector.quantize_mx(out=z2q[:].bitcast(FP8X4), scales=z2s[:], in_=z2g[:].rearrange("p c t -> p (c t)"))
-        for i in range(1, len(pieces)):
+        smaller(1)
+        gate(0)
+        for i in range(2, len(pieces)):
             if i + 1 < len(pieces):
                 fetch(i + 1)
             larger(i)
             differ(i - 1)
             smaller(i)
-            if i > 1:
-                gate(i - 2)
-        differ(4)
-        gate(3)
+            gate(i - 1)
         weave(nc.scalar.copy, 0)
+        differ(4)
         gate(4)
         weave(nc.vector.tensor_copy, 1)
         zq = new("zq", [P, S], U32)
         zs = new("zs", [P, S], U8)
         nc.vector.quantize_mx(out=zq[:].bitcast(FP8X4), scales=zs[:], in_=zg[:].rearrange("p c t -> p (c t)"))
 
-        s_ps = [ps.tile([P, 2, V], F32, name=f"s_ps{h}") for h in range(2)]
+        s_ps = [ps.tile([P, V], F32, name=f"s_ps{t}") for t in range(4)]
         s_sb = [new(f"s_sb{t}", [P, V], F32) for t in range(4)]
         for t in range(4):
-            product(s_ps[t % 2][:, t // 2, :], zq, zs, t, z2q, z2s)
+            product(s_ps[t][:], block(zq, t), block(zs, t), z2q, z2s)
         for t in range(4):
-            nc.vector.tensor_scalar(s_sb[t][:], s_ps[t % 2][:, t // 2, :], 0.0625, None, ALU.mult)
+            nc.vector.tensor_scalar(s_sb[t][:], s_ps[t][:], 0.0625, None, ALU.mult)
 
         grouped = new("grouped", [P, U, 4], BF16)
         words = new("words", [P, U], I32)

@@ -40,7 +40,7 @@ def tile_picked_kqghardrangepage_none_po_kernel(tc, x_words, x_scales, w1_words,
                 queues[q].dma_start(plane[32 * q : 32 * q + 4, :].bitcast(I32), src[0, 4 * q : 4 * q + 4, :].bitcast(I32))
 
         xs = new("xs", [P, T], U8, "slot0")
-        w2s_raw = new("w2s_raw", [P, H], U8, "slot3")
+        w2s_raw = new("w2s_raw", [P, H], U8, "xa")
         w1s_raw = new("w1s_raw", [P, H], U8, "ends")
         nc.vector.memset(xs[:, : T // 2].bitcast(I32), 0)
         nc.gpsimd.memset(xs[:, T // 2 :].bitcast(I32), 0)
@@ -67,9 +67,9 @@ def tile_picked_kqghardrangepage_none_po_kernel(tc, x_words, x_scales, w1_words,
         bw = [new(f"bw{t}", [P, 2 * V], F32) for t in range(4)]
         aw = [new(f"aw{t}", [P, (2 * S if t < 3 else S) + 16], F32) for t in range(4)]
         for t in range(4):
-            nc.gpsimd.memset(bw[t][:, V:], 0.0)
+            nc.vector.memset(bw[t][:, V:], 0.0)
         for t in range(4):
-            nc.gpsimd.memset(aw[t][:, S:], 0.0)
+            nc.vector.memset(aw[t][:, S:], 0.0)
         gb_t = new("gb_t", [P, 4], F32)
         nc.sync.dma_start(gb_t[:], gb.rearrange("(p t) o -> p (t o)", t=4))
         ga_t = new("ga_t", [P, 4], F32)
@@ -84,13 +84,13 @@ def tile_picked_kqghardrangepage_none_po_kernel(tc, x_words, x_scales, w1_words,
         def deal_bytes(dst, src):
             nc.vector.tensor_copy(dst[:].rearrange("p (t m) -> p t m", t=4), src[:].rearrange("p (m t) -> p t m", t=4))
 
-        w2 = new("w2", [P, H], I32)
+        w2 = new("w2", [P, H], I32, "slot3")
         deal(w2, w2_raw)
-        xb_s = new("xb_s", [P, V], U8)
+        xb_s = new("xb_s", [P, V], U8, "w1_second")
         nc.vector.tensor_copy(xb_s[:], xs[:].indirect(two_l[:]))
         xa_s = new("xa_s", [P, S], U8)
         nc.vector.tensor_copy(xa_s[:], xs[:].indirect(offs_l[:]))
-        xb = new("xb", [P, V], U32)
+        xb = new("xb", [P, V], U32, "w1s")
         nc.vector.tensor_copy(xb[:], xw[:].bitcast(U32).indirect(two_l[:]))
         w2s = new("w2s", [P, H], U8)
         deal_bytes(w2s, w2s_raw)
@@ -129,8 +129,7 @@ def tile_picked_kqghardrangepage_none_po_kernel(tc, x_words, x_scales, w1_words,
         for t in range(2):
             nc.vector.tensor_copy(aw[t][:, :S], a_ps[t][:])
 
-        u = new("u", [P, 4, V], F32)
-        z2b = new("z2b", [P, 4, V], BF16, "mx1")
+        u = new("u", [P, 4, V], F32, "mx1")
         top, low = {}, {}
 
         def of_two(h):
@@ -149,10 +148,6 @@ def tile_picked_kqghardrangepage_none_po_kernel(tc, x_words, x_scales, w1_words,
 
         def spread(h):
             nc.vector.scalar_tensor_tensor(u[:, 2 * h : 2 * h + 2, :], low[h][:], -0.5, top[h][:], ALU.mult, ALU.add)
-
-        def weigh(h):
-            for t in (2 * h, 2 * h + 1):
-                nc.vector.tensor_scalar(z2b[:, t, :], u[:, t, :], gb_t[:, t : t + 1], None, ALU.mult)
 
         mx, mn, sg, df, mb = {}, {}, {}, {}, {}
         zb = new("zb", [P, 4, S], BF16)
@@ -193,45 +188,51 @@ def tile_picked_kqghardrangepage_none_po_kernel(tc, x_words, x_scales, w1_words,
         def gate(i):
             t, lo_col, hi_col = pieces[i]
             nc.vector.scalar_tensor_tensor(
-                zb[:, t, lo_col:hi_col],
-                df[i][:],
+                zb[:, t, :].rearrange("p (s m) -> p m s", s=4)[:, lo_col // 4 : hi_col // 4, :],
+                df[i][:].rearrange("p (m s) -> p m s", s=4),
                 ga_t[:, t : t + 1],
-                sg[i][:],
+                sg[i][:].rearrange("p (m s) -> p m s", s=4),
                 ALU.mult,
                 ALU.mult,
             )
 
         def weave(copy, h):
             copy(
-                zg[:].rearrange("p (s h m) t -> p h s m t", s=4, h=2)[:, h],
-                zb[:].rearrange("p t (h m s) -> p h s m t", s=4, h=2)[:, h],
+                zg[:].rearrange("p (s h c i) t -> p h s c t i", s=4, h=2, i=4)[:, h],
+                zb[:].rearrange("p t (s h c i) -> p h s c t i", s=4, h=2, i=4)[:, h],
             )
 
         of_three(0, of_two(0))
         spread(0)
         ends = of_two(1)
-        weigh(0)
         of_three(1, ends)
         fetch(0)
         fetch(1)
         larger(0)
         spread(1)
         smaller(0)
-        weigh(1)
+        nc.vector.tensor_tensor(
+            z2g[:].rearrange("p (c i) t -> p c t i", i=4),
+            u[:].rearrange("p t (c i) -> p c t i", i=4),
+            gb_t[:].unsqueeze(1).unsqueeze(3).broadcast_to([P, V // 4, 4, 4]),
+            ALU.mult,
+        )
         differ(0)
-        nc.vector.tensor_copy(z2g[:], z2b[:].rearrange("p t v -> p v t"))
         fetch(2)
         larger(1)
         nc.vector.quantize_mx(out=z2q[:].bitcast(FP8X4), scales=z2s[:], in_=z2g[:].rearrange("p c t -> p (c t)"))
         smaller(1)
         gate(0)
-        for i in range(2, len(pieces)):
-            if i + 1 < len(pieces):
-                fetch(i + 1)
+        for i in (2, 3):
+            fetch(i + 1)
             larger(i)
             differ(i - 1)
             smaller(i)
             gate(i - 1)
+        differ(3)
+        larger(4)
+        smaller(4)
+        gate(3)
         weave(nc.scalar.copy, 0)
         differ(4)
         gate(4)
@@ -240,26 +241,36 @@ def tile_picked_kqghardrangepage_none_po_kernel(tc, x_words, x_scales, w1_words,
         zs = new("zs", [P, S], U8)
         nc.vector.quantize_mx(out=zq[:].bitcast(FP8X4), scales=zs[:], in_=zg[:].rearrange("p c t -> p (c t)"))
 
-        s_ps = [ps.tile([P, V], F32, name=f"s_ps{t}") for t in range(4)]
-        s_sb = [new(f"s_sb{t}", [P, V], F32) for t in range(4)]
-        for t in range(4):
+        order = (2, 0, 1, 3)
+        s_ps = {t: ps.tile([P, V], F32, name=f"s_ps{t}") for t in order}
+        s_sb = {}
+        for t in order:
             product(s_ps[t][:], block(zq, t), block(zs, t), z2q, z2s)
-        for t in range(4):
+
+        def scale_down(t, tag=None):
+            s_sb[t] = new(f"s_sb{t}", [P, V], F32, tag)
             nc.vector.tensor_scalar(s_sb[t][:], s_ps[t][:], 0.0625, None, ALU.mult)
+
+        for t in order[:3]:
+            scale_down(t)
 
         grouped = new("grouped", [P, U, 4], BF16)
         words = new("words", [P, U], I32)
         scales = new("scales", [P, U], U8)
         half = U // 2
-        for t in range(4):
+        for t in order:
             nc.scalar.activation(page[t][:].indirect(n4_l[:]), s_sb[t][:], ACT.Copy)
             nc.sync.dma_start(out_rows[:, t, :], page[t][:])
             if t < 3:
                 nc.vector.tensor_copy(grouped[:, :, t], page[t][:])
+            if t == 2:
+                scale_down(3, "s_sb2")
         out_words = as_words(out_1)
+        nc.vector.tensor_copy(grouped[:, :half, 3], page[3][:, :half])
+        nc.vector.tensor_copy(grouped[:, half:576, 3], page[3][:, half:576])
+        nc.scalar.copy(grouped[:, 576:, 3], page[3][:, 576:])
         for h in range(2):
             cols = slice(half * h, half * (h + 1))
-            nc.vector.tensor_copy(grouped[:, cols, 3], page[3][:, cols])
             nc.vector.quantize_mx(out=words[:, cols].bitcast(FP8X4), scales=scales[:, cols], in_=grouped[:, cols, :].rearrange("p c t -> p (c t)"))
             nc.sync.dma_start(out_words[:, cols], words[:, cols])
         for q in range(4):

@@ -196,10 +196,10 @@ def tile_picked_kqghardrangepage_none_po_kernel(tc, x_words, x_scales, w1_words,
                 ALU.mult,
             )
 
-        def weave(copy, h):
+        def weave(copy, h, blocks):
             copy(
-                zg[:].rearrange("p (s h c i) t -> p h s c t i", s=4, h=2, i=4)[:, h],
-                zb[:].rearrange("p t (s h c i) -> p h s c t i", s=4, h=2, i=4)[:, h],
+                zg[:].rearrange("p (s h c i) t -> p h s c t i", s=4, h=2, i=4)[:, h, blocks],
+                zb[:].rearrange("p t (s h c i) -> p h s c t i", s=4, h=2, i=4)[:, h, blocks],
             )
 
         of_three(0, of_two(0))
@@ -233,15 +233,19 @@ def tile_picked_kqghardrangepage_none_po_kernel(tc, x_words, x_scales, w1_words,
         larger(4)
         smaller(4)
         gate(3)
-        weave(nc.scalar.copy, 0)
+        first, rest = slice(0, 1), slice(1, 4)
+        weave(nc.scalar.copy, 0, first)
+        weave(nc.scalar.copy, 0, rest)
         differ(4)
         gate(4)
-        weave(nc.vector.tensor_copy, 1)
         zq = new("zq", [P, S], U32)
         zs = new("zs", [P, S], U8)
-        nc.vector.quantize_mx(out=zq[:].bitcast(FP8X4), scales=zs[:], in_=zg[:].rearrange("p c t -> p (c t)"))
+        for blocks in (first, rest):
+            cols = slice(P * blocks.start, P * blocks.stop)
+            weave(nc.vector.tensor_copy, 1, blocks)
+            nc.vector.quantize_mx(out=zq[:, cols].bitcast(FP8X4), scales=zs[:, cols], in_=zg[:, cols, :].rearrange("p c t -> p (c t)"))
 
-        order = (2, 0, 1, 3)
+        order = (0, 2, 3, 1)
         s_ps = {t: ps.tile([P, V], F32, name=f"s_ps{t}") for t in order}
         s_sb = {}
         for t in order:
@@ -251,7 +255,9 @@ def tile_picked_kqghardrangepage_none_po_kernel(tc, x_words, x_scales, w1_words,
             s_sb[t] = new(f"s_sb{t}", [P, V], F32, tag)
             nc.vector.tensor_scalar(s_sb[t][:], s_ps[t][:], 0.0625, None, ALU.mult)
 
-        for t in order[:3]:
+        s_sb[0] = new("s_sb0", [P, V], F32)
+        nc.scalar.activation(s_sb[0][:], s_ps[0][:], ACT.Copy, scale=0.0625)
+        for t in order[1:3]:
             scale_down(t)
 
         grouped = new("grouped", [P, U, 4], BF16)
@@ -261,14 +267,14 @@ def tile_picked_kqghardrangepage_none_po_kernel(tc, x_words, x_scales, w1_words,
         for t in order:
             nc.scalar.activation(page[t][:].indirect(n4_l[:]), s_sb[t][:], ACT.Copy)
             nc.sync.dma_start(out_rows[:, t, :], page[t][:])
-            if t < 3:
+            if t != 1:
                 nc.vector.tensor_copy(grouped[:, :, t], page[t][:])
-            if t == 2:
-                scale_down(3, "s_sb2")
+            if t == 0:
+                scale_down(1, "s_sb0")
         out_words = as_words(out_1)
-        nc.vector.tensor_copy(grouped[:, :half, 3], page[3][:, :half])
-        nc.vector.tensor_copy(grouped[:, half:576, 3], page[3][:, half:576])
-        nc.scalar.copy(grouped[:, 576:, 3], page[3][:, 576:])
+        nc.vector.tensor_copy(grouped[:, :half, 1], page[1][:, :half])
+        nc.vector.tensor_copy(grouped[:, half:576, 1], page[1][:, half:576])
+        nc.scalar.copy(grouped[:, 576:, 1], page[1][:, 576:])
         for h in range(2):
             cols = slice(half * h, half * (h + 1))
             nc.vector.quantize_mx(out=words[:, cols].bitcast(FP8X4), scales=scales[:, cols], in_=grouped[:, cols, :].rearrange("p c t -> p (c t)"))

@@ -13,12 +13,24 @@ ALU = mybir.AluOpType
 ACT = mybir.ActivationFunctionType
 
 P = 128
-T, S, V, H, U = 2048, 512, 256, 512, 1024
-FLOPS = 2 * 512 * H * S + 2 * 512 * H * V + 2 * H * S * V
+PACK = 4
+LIST_ROWS = 16
+K, T, S, V, H, U = 512, 2048, 512, 256, 512, 1024
+FLOPS = 2 * K * H * S + 2 * K * H * V + 2 * H * S * V
+
+PIECES = [(0, 0, S), (1, 0, S), (2, 0, S), (3, 0, S // 2), (3, S // 2, S)]
+
+PAGE_ORDER = (0, 2, 3, 1)
+
+VECTOR_COLUMNS = 576
 
 
 def as_words(packed):
     return packed[0].rearrange("p n t -> p (n t)").bitcast(I32)
+
+
+def block(dealt, t):
+    return dealt[:, P * t : P * (t + 1)]
 
 
 def tile_picked_kqghardrangepage_none_po_kernel(tc, x_words, x_scales, w1_words, w1_scales, w2_words, w2_scales, ga, gb, mem, offs, two, n1, n2, n3, n4, out_0, out_1, out_2):
@@ -27,200 +39,195 @@ def tile_picked_kqghardrangepage_none_po_kernel(tc, x_words, x_scales, w1_words,
         sb = ctx.enter_context(tc.tile_pool(name="sb", bufs=1))
         ps = ctx.enter_context(tc.psum_pool(name="ps", bufs=1))
 
-        def new(name, shape, dtype, tag=None):
-            return sb.tile(shape, dtype, name=name, tag=tag or name, align_bytes=64)
+        def new(name, shape, dtype, slot=None):
+            return sb.tile(shape, dtype, name=name, tag=slot or name, align_bytes=64)
 
         def load_list(name, src):
-            t = sb.tile(list(src.shape), U16, name=name)
-            nc.sync.dma_start(t[:], src)
-            return t
+            offsets = sb.tile(list(src.shape), U16, name=name)
+            nc.sync.dma_start(offsets[:], src)
+            return offsets
 
-        def load_scales(queues, plane, src):
+        def load_scales(dst, src):
             for q in range(4):
-                queues[q].dma_start(plane[32 * q : 32 * q + 4, :].bitcast(I32), src[0, 4 * q : 4 * q + 4, :].bitcast(I32))
+                nc.sync.dma_start(dst[32 * q : 32 * q + 4, :].bitcast(I32), src[0, 4 * q : 4 * q + 4, :].bitcast(I32))
 
-        xs = new("xs", [P, T], U8, "slot0")
-        w2s_raw = new("w2s_raw", [P, H], U8, "xa")
-        w1s_raw = new("w1s_raw", [P, H], U8, "ends")
-        nc.vector.memset(xs[:, : T // 2].bitcast(I32), 0)
-        nc.gpsimd.memset(xs[:, T // 2 :].bitcast(I32), 0)
-        for plane in (w2s_raw, w1s_raw):
-            nc.gpsimd.memset(plane[:].bitcast(I32), 0)
-        warm = new("warm", [P, 2], F32)
-        nc.vector.memset(warm[:, 0:1], 0.0)
+        def product(out, lhs_words, lhs_scales, rhs_words, rhs_scales):
+            nc.tensor.matmul_mx(out=out, lhsT=lhs_words.bitcast(FP8X4), lhsT_scale=lhs_scales, rhs=rhs_words[:].bitcast(FP8X4), rhs_scale=rhs_scales[:], start=True, stop=True)
 
-        nc.scalar.activation(warm[:, 1:2], warm[:, 0:1], ACT.Sigmoid)
+        def quantize(words_out, scales_out, woven):
+            nc.vector.quantize_mx(out=words_out.bitcast(FP8X4), scales=scales_out, in_=woven.rearrange("p c t -> p (c t)"))
+
+        x_sc = new("x_sc", [P, T], U8, "page0")
+        w2_sc_raw = new("w2_sc_raw", [P, H], U8, "xa")
+        w1_sc_raw = new("w1_sc_raw", [P, H], U8, "ends")
+        nc.vector.memset(x_sc[:, : T // 2].bitcast(I32), 0)
+        nc.gpsimd.memset(x_sc[:, T // 2 :].bitcast(I32), 0)
+        for raw in (w2_sc_raw, w1_sc_raw):
+            nc.gpsimd.memset(raw[:].bitcast(I32), 0)
+
         two_l = load_list("two_l", two)
         offs_l = load_list("offs_l", offs)
-        w2_raw = new("w2_raw", [P, H], I32, "slot1")
+        w2_raw = new("w2_raw", [P, H], I32, "page1")
         nc.sync.dma_start(w2_raw[:], as_words(w2_words))
-        load_scales([nc.sync] * 4, xs, x_scales)
-        xw = new("xw", [P, T], I32, "slot2")
-        nc.sync.dma_start(xw[:], as_words(x_words))
-        load_scales([nc.sync] * 4, w2s_raw, w2_scales)
+        load_scales(x_sc, x_scales)
+        x_wd = new("x_wd", [P, T], I32, "page2")
+        nc.sync.dma_start(x_wd[:], as_words(x_words))
+        load_scales(w2_sc_raw, w2_scales)
         n2_l = load_list("n2_l", n2)
         n3_l = load_list("n3_l", n3)
         w1_raw = new("w1_raw", [P, H], I32)
         nc.sync.dma_start(w1_raw[:], as_words(w1_words))
-        load_scales([nc.sync] * 4, w1s_raw, w1_scales)
+        load_scales(w1_sc_raw, w1_scales)
         n1_l = load_list("n1_l", n1)
-        bw = [new(f"bw{t}", [P, 2 * V], F32) for t in range(4)]
-        aw = [new(f"aw{t}", [P, (2 * S if t < 3 else S) + 16], F32) for t in range(4)]
-        for t in range(4):
-            nc.vector.memset(bw[t][:, V:], 0.0)
-        for t in range(4):
-            nc.vector.memset(aw[t][:, S:], 0.0)
-        gb_t = new("gb_t", [P, 4], F32)
-        nc.sync.dma_start(gb_t[:], gb.rearrange("(p t) o -> p (t o)", t=4))
-        ga_t = new("ga_t", [P, 4], F32)
-        nc.sync.dma_start(ga_t[:], ga.rearrange("(p t) o -> p (t o)", t=4))
+
+        b_win = [new(f"b_win{t}", [P, 2 * V], F32) for t in range(PACK)]
+        a_win = [new(f"a_win{t}", [P, (2 * S if t < PACK - 1 else S) + LIST_ROWS], F32) for t in range(PACK)]
+        for t in range(PACK):
+            nc.vector.memset(b_win[t][:, V:], 0.0)
+        warm = new("warm", [P, 1], F32)
+        nc.scalar.activation(warm[:], b_win[0][:, V : V + 1], ACT.Sigmoid)
+        for t in range(PACK):
+            nc.vector.memset(a_win[t][:, S:], 0.0)
+
+        gb_t = new("gb_t", [P, PACK], F32)
+        nc.sync.dma_start(gb_t[:], gb.rearrange("(p t) o -> p (t o)", t=PACK))
+        ga_t = new("ga_t", [P, PACK], F32)
+        nc.sync.dma_start(ga_t[:], ga.rearrange("(p t) o -> p (t o)", t=PACK))
         n4_l = load_list("n4_l", n4)
-        mem_rows = mem.rearrange("(p t) u -> p t u", t=4)
-        out_rows = out_0.rearrange("(p t) u -> p t u", t=4)
 
-        def deal(dst, src):
-            nc.vector.tensor_copy(dst[:].rearrange("p (t m) -> p m t", t=4), src[:].rearrange("p (m t) -> p m t", t=4))
+        def deal_scales(dst, src):
+            nc.vector.tensor_copy(dst[:].rearrange("p (t m) -> p t m", t=PACK), src[:].rearrange("p (m t) -> p t m", t=PACK))
 
-        def deal_bytes(dst, src):
-            nc.vector.tensor_copy(dst[:].rearrange("p (t m) -> p t m", t=4), src[:].rearrange("p (m t) -> p t m", t=4))
-
-        w2 = new("w2", [P, H], I32, "slot3")
-        deal(w2, w2_raw)
-        xb_s = new("xb_s", [P, V], U8, "w1_second")
-        nc.vector.tensor_copy(xb_s[:], xs[:].indirect(two_l[:]))
-        xa_s = new("xa_s", [P, S], U8)
-        nc.vector.tensor_copy(xa_s[:], xs[:].indirect(offs_l[:]))
-        xb = new("xb", [P, V], U32, "w1s")
-        nc.vector.tensor_copy(xb[:], xw[:].bitcast(U32).indirect(two_l[:]))
-        w2s = new("w2s", [P, H], U8)
-        deal_bytes(w2s, w2s_raw)
-
-        def block(tile_, t):
-            return tile_[:, P * t : P * (t + 1)]
-
-        def product(out, lhs, lhs_s, rhs, rhs_s):
-            nc.tensor.matmul_mx(out=out, lhsT=lhs.bitcast(FP8X4), lhsT_scale=lhs_s, rhs=rhs[:].bitcast(FP8X4), rhs_scale=rhs_s[:], start=True, stop=True)
+        w2 = new("w2", [P, H], I32, "page3")
+        nc.vector.tensor_copy(w2[:].rearrange("p (t m) -> p m t", t=PACK), w2_raw[:].rearrange("p (m t) -> p m t", t=PACK))
+        xb_sc = new("xb_sc", [P, V], U8, "w1_second")
+        nc.vector.tensor_copy(xb_sc[:], x_sc[:].indirect(two_l[:]))
+        xa_sc = new("xa_sc", [P, S], U8)
+        nc.vector.tensor_copy(xa_sc[:], x_sc[:].indirect(offs_l[:]))
+        xb = new("xb", [P, V], U32, "w1_sc")
+        nc.vector.tensor_copy(xb[:], x_wd[:].bitcast(U32).indirect(two_l[:]))
+        w2_sc = new("w2_sc", [P, H], U8)
+        deal_scales(w2_sc, w2_sc_raw)
 
         b_ps = [ps.tile([P, 2, V], F32, name=f"b_ps{h}") for h in range(2)]
-        for t in range(4):
-            product(b_ps[t // 2][:, t % 2, :], block(w2, t), block(w2s, t), xb, xb_s)
+        for t in range(PACK):
+            product(b_ps[t // 2][:, t % 2, :], block(w2, t), block(w2_sc, t), xb, xb_sc)
 
         xa = new("xa", [P, S], U32)
-        nc.vector.tensor_copy(xa[:], xw[:].bitcast(U32).indirect(offs_l[:]))
-        w1s = new("w1s", [P, H], U8)
-        deal_bytes(w1s, w1s_raw)
+        nc.vector.tensor_copy(xa[:], x_wd[:].bitcast(U32).indirect(offs_l[:]))
+        for t in (2, 3):
+            nc.vector.tensor_copy(b_win[t][:, :V], b_ps[1][:, t % 2, :])
+        w1_sc = new("w1_sc", [P, H], U8)
+        deal_scales(w1_sc, w1_sc_raw)
         w1 = [new("w1_first", [P, H // 2], I32, "ends"), new("w1_second", [P, H // 2], I32)]
         for h in range(2):
-            nc.vector.tensor_copy(w1[h][:].rearrange("p (t m) -> p m t", t=2), w1_raw[:].rearrange("p (m t) -> p m t", t=4)[:, :, 2 * h : 2 * h + 2])
+            nc.vector.tensor_copy(w1[h][:].rearrange("p (t m) -> p m t", t=2), w1_raw[:].rearrange("p (m t) -> p m t", t=PACK)[:, :, 2 * h : 2 * h + 2])
         a_ps = [ps.tile([P, S], F32, name=f"a_ps{t}") for t in range(2)]
         for t in range(2):
-            product(a_ps[t][:], block(w1[0], t), block(w1s, t), xa, xa_s)
+            product(a_ps[t][:], block(w1[0], t), block(w1_sc, t), xa, xa_sc)
 
-        page = [new(f"page{t}", [P, U], F32, f"slot{t}") for t in range(4)]
-        for t in range(4):
+        mem_rows = mem.rearrange("(p t) u -> p t u", t=PACK)
+        page = [new(f"page{t}", [P, U], F32) for t in range(PACK)]
+        for t in range(PACK):
             nc.sync.dma_start(page[t][:], mem_rows[:, t, :])
 
         pa = [new(f"pa{h}", [P, 2, V], F32) for h in range(2)]
         pb = [new(f"pb{h}", [P, 2, V], F32) for h in range(2)]
-        for t in range(4):
-            nc.scalar.copy(bw[t][:, :V], b_ps[t // 2][:, t % 2, :])
-            nc.scalar.activation(pa[t // 2][:, t % 2, :], bw[t][:].indirect(n2_l[:]), ACT.Copy)
-            nc.scalar.activation(pb[t // 2][:, t % 2, :], bw[t][:].indirect(n3_l[:]), ACT.Copy)
+        for t in range(PACK):
+            if t < 2:
+                nc.scalar.copy(b_win[t][:, :V], b_ps[0][:, t, :])
+            nc.scalar.activation(pa[t // 2][:, t % 2, :], b_win[t][:].indirect(n2_l[:]), ACT.Copy)
+            nc.scalar.activation(pb[t // 2][:, t % 2, :], b_win[t][:].indirect(n3_l[:]), ACT.Copy)
         for t in range(2):
-            nc.vector.tensor_copy(aw[t][:, :S], a_ps[t][:])
+            nc.vector.tensor_copy(a_win[t][:, :S], a_ps[t][:])
 
-        u = new("u", [P, 4, V], F32, "mx1")
+        spread = new("spread", [P, PACK, V], F32)
         top, low = {}, {}
 
-        def of_two(h):
+        def ends_of_three(h):
             ends = new(f"ends{h}", [P, 2, 2, V], F32, "ends")
             nc.vector.tensor_tensor(ends[:, 0], pa[h][:], pb[h][:], ALU.min)
             nc.vector.tensor_tensor(ends[:, 1], pa[h][:], pb[h][:], ALU.max)
-            return ends
-
-        def of_three(h, ends):
             low[h] = new(f"low{h}", [P, 2, V], F32, "mn" if h else None)
             top[h] = new(f"top{h}", [P, 2, V], F32)
             nc.vector.tensor_tensor(low[h][:], ends[:, 0], b_ps[h][:], ALU.min)
             nc.vector.tensor_tensor(top[h][:], ends[:, 1], b_ps[h][:], ALU.max)
             a_ps.append(ps.tile([P, S], F32, name=f"a_ps{2 + h}", tag=f"b_ps{h}"))
-            product(a_ps[2 + h][:], block(w1[1], h), block(w1s, 2 + h), xa, xa_s)
+            product(a_ps[2 + h][:], block(w1[1], h), block(w1_sc, 2 + h), xa, xa_sc)
 
-        def spread(h):
-            nc.vector.scalar_tensor_tensor(u[:, 2 * h : 2 * h + 2, :], low[h][:], -0.5, top[h][:], ALU.mult, ALU.add)
+        def spread_of(h):
+            nc.vector.scalar_tensor_tensor(spread[:, 2 * h : 2 * h + 2, :], low[h][:], -0.5, top[h][:], ALU.mult, ALU.add)
 
-        mx, mn, sg, df, mb = {}, {}, {}, {}, {}
-        zb = new("zb", [P, 4, S], BF16)
-        zg = new("zg", [P, S, 4], BF16)
-        z2g = new("z2g", [P, V, 4], BF16)
-        z2q = new("z2q", [P, V], U32)
-        z2s = new("z2s", [P, V], U8)
-        pieces = [(0, 0, S), (1, 0, S), (2, 0, S), (3, 0, S // 2), (3, S // 2, S)]
+        mb, mx, mn, sg, diff = {}, {}, {}, {}, {}
+        z_bf = new("z_bf", [P, PACK, S], BF16)
+        z_woven = new("z_woven", [P, S, PACK], BF16)
+        z2_woven = new("z2_woven", [P, V, PACK], BF16)
+        z2_wd = new("z2_wd", [P, V], U32)
+        z2_sc = new("z2_sc", [P, V], U8)
 
-        larger_slot = ["ends", "mx1", "df0", "df1", "df2"]
+        mx_slot = ["ends", "spread", "diff0", "diff1", "diff2"]
 
         def fetch(i):
-            t, lo_col, hi_col = pieces[i]
-            if t >= 2 and lo_col == 0:
-                nc.scalar.copy(aw[t][:, :S], a_ps[t][:])
-            mb[i] = new(f"mb{i}", [P, 2 * (hi_col - lo_col)], F32, larger_slot[i - 2] if i >= 2 else None)
-            nc.scalar.activation(mb[i][:], aw[t][:].indirect(n1_l[:, lo_col // 8 : hi_col // 8]), ACT.Copy)
+            t, first, end = PIECES[i]
+            if t >= 2 and first == 0:
+                nc.scalar.copy(a_win[t][:, :S], a_ps[t][:])
+            mb[i] = new(f"mb{i}", [P, 2 * (end - first)], F32, mx_slot[i - 2] if i >= 2 else None)
+            nc.scalar.activation(mb[i][:], a_win[t][:].indirect(n1_l[:, 2 * first // LIST_ROWS : 2 * end // LIST_ROWS]), ACT.Copy)
 
         def larger(i):
-            t, lo_col, hi_col = pieces[i]
-            pairs = mb[i][:].rearrange("p (j e) -> p j e", e=2)
-            mx[i] = new(f"mx{i}", [P, hi_col - lo_col], F32, larger_slot[i])
-            nc.vector.tensor_tensor(mx[i][:], pairs[:, :, 0], pairs[:, :, 1], ALU.max)
-            sg[i] = new(f"sg{i}", [P, hi_col - lo_col], F32)
+            t, first, end = PIECES[i]
+            members = mb[i][:].rearrange("p (j e) -> p j e", e=2)
+            mx[i] = new(f"mx{i}", [P, end - first], F32, mx_slot[i])
+            nc.vector.tensor_tensor(mx[i][:], members[:, :, 0], members[:, :, 1], ALU.max)
+            sg[i] = new(f"sg{i}", [P, end - first], F32)
             nc.scalar.activation(sg[i][:], mx[i][:], ACT.Sigmoid)
 
         def smaller(i):
-            t, lo_col, hi_col = pieces[i]
-            pairs = mb[i][:].rearrange("p (j e) -> p j e", e=2)
-            mn[i] = new(f"mn{i}", [P, hi_col - lo_col], F32, "mn")
-            nc.vector.tensor_tensor(mn[i][:], pairs[:, :, 0], pairs[:, :, 1], ALU.min)
+            t, first, end = PIECES[i]
+            members = mb[i][:].rearrange("p (j e) -> p j e", e=2)
+            mn[i] = new(f"mn{i}", [P, end - first], F32, "mn")
+            nc.vector.tensor_tensor(mn[i][:], members[:, :, 0], members[:, :, 1], ALU.min)
 
         def differ(i):
-            t, lo_col, hi_col = pieces[i]
-            df[i] = new(f"df{i}", [P, hi_col - lo_col], F32)
-            nc.vector.tensor_tensor(df[i][:], aw[t][:, lo_col:hi_col], mn[i][:], ALU.subtract)
+            t, first, end = PIECES[i]
+            diff[i] = new(f"diff{i}", [P, end - first], F32)
+            nc.vector.tensor_tensor(diff[i][:], a_win[t][:, first:end], mn[i][:], ALU.subtract)
 
         def gate(i):
-            t, lo_col, hi_col = pieces[i]
+            t, first, end = PIECES[i]
             nc.vector.scalar_tensor_tensor(
-                zb[:, t, :].rearrange("p (s m) -> p m s", s=4)[:, lo_col // 4 : hi_col // 4, :],
-                df[i][:].rearrange("p (m s) -> p m s", s=4),
+                z_bf[:, t, :].rearrange("p (s m) -> p m s", s=PACK)[:, first // PACK : end // PACK, :],
+                diff[i][:].rearrange("p (m s) -> p m s", s=PACK),
                 ga_t[:, t : t + 1],
-                sg[i][:].rearrange("p (m s) -> p m s", s=4),
+                sg[i][:].rearrange("p (m s) -> p m s", s=PACK),
                 ALU.mult,
                 ALU.mult,
             )
 
-        def weave(copy, h, blocks):
+        def weave_z(copy, h, blocks):
             copy(
-                zg[:].rearrange("p (s h c i) t -> p h s c t i", s=4, h=2, i=4)[:, h, blocks],
-                zb[:].rearrange("p t (s h c i) -> p h s c t i", s=4, h=2, i=4)[:, h, blocks],
+                z_woven[:].rearrange("p (s h c i) t -> p h s c t i", s=PACK, h=2, i=4)[:, h, blocks],
+                z_bf[:].rearrange("p t (s h c i) -> p h s c t i", s=PACK, h=2, i=4)[:, h, blocks],
             )
 
-        of_three(0, of_two(0))
-        spread(0)
-        ends = of_two(1)
-        of_three(1, ends)
+        ends_of_three(0)
+        spread_of(0)
+        ends_of_three(1)
         fetch(0)
         fetch(1)
         larger(0)
-        spread(1)
+        spread_of(1)
         smaller(0)
         nc.vector.tensor_tensor(
-            z2g[:].rearrange("p (c i) t -> p c t i", i=4),
-            u[:].rearrange("p t (c i) -> p c t i", i=4),
-            gb_t[:].unsqueeze(1).unsqueeze(3).broadcast_to([P, V // 4, 4, 4]),
+            z2_woven[:].rearrange("p (c i) t -> p c t i", i=4),
+            spread[:].rearrange("p t (c i) -> p c t i", i=4),
+            gb_t[:].unsqueeze(1).unsqueeze(3).broadcast_to([P, V // 4, PACK, 4]),
             ALU.mult,
         )
         differ(0)
         fetch(2)
         larger(1)
-        nc.vector.quantize_mx(out=z2q[:].bitcast(FP8X4), scales=z2s[:], in_=z2g[:].rearrange("p c t -> p (c t)"))
+        quantize(z2_wd[:], z2_sc[:], z2_woven[:])
         smaller(1)
         gate(0)
         for i in (2, 3):
@@ -233,52 +240,55 @@ def tile_picked_kqghardrangepage_none_po_kernel(tc, x_words, x_scales, w1_words,
         larger(4)
         smaller(4)
         gate(3)
-        first, rest = slice(0, 1), slice(1, 4)
-        weave(nc.scalar.copy, 0, first)
-        weave(nc.scalar.copy, 0, rest)
+        weave_z(nc.scalar.copy, 0, slice(0, 1))
+        weave_z(nc.scalar.copy, 0, slice(1, PACK))
         differ(4)
         gate(4)
-        zq = new("zq", [P, S], U32)
-        zs = new("zs", [P, S], U8)
-        for blocks in (first, rest):
-            cols = slice(P * blocks.start, P * blocks.stop)
-            weave(nc.vector.tensor_copy, 1, blocks)
-            nc.vector.quantize_mx(out=zq[:, cols].bitcast(FP8X4), scales=zs[:, cols], in_=zg[:, cols, :].rearrange("p c t -> p (c t)"))
+        z_wd = new("z_wd", [P, S], U32)
+        z_sc = new("z_sc", [P, S], U8)
+        for step in range(PACK + 1):
+            if step < PACK:
+                weave_z(nc.vector.tensor_copy, 1, slice(PAGE_ORDER[step], PAGE_ORDER[step] + 1))
+            if step > 0:
+                t = PAGE_ORDER[step - 1]
+                quantize(block(z_wd, t), block(z_sc, t), z_woven[:, P * t : P * (t + 1), :])
 
-        order = (0, 2, 3, 1)
-        s_ps = {t: ps.tile([P, V], F32, name=f"s_ps{t}") for t in order}
+        s_ps = {t: ps.tile([P, V], F32, name=f"s_ps{t}") for t in PAGE_ORDER}
         s_sb = {}
-        for t in order:
-            product(s_ps[t][:], block(zq, t), block(zs, t), z2q, z2s)
+        for t in PAGE_ORDER:
+            product(s_ps[t][:], block(z_wd, t), block(z_sc, t), z2_wd, z2_sc)
 
-        def scale_down(t, tag=None):
-            s_sb[t] = new(f"s_sb{t}", [P, V], F32, tag)
+        def scale_down(t, slot=None):
+            s_sb[t] = new(f"s_sb{t}", [P, V], F32, slot)
             nc.vector.tensor_scalar(s_sb[t][:], s_ps[t][:], 0.0625, None, ALU.mult)
 
-        s_sb[0] = new("s_sb0", [P, V], F32)
-        nc.scalar.activation(s_sb[0][:], s_ps[0][:], ACT.Copy, scale=0.0625)
-        for t in order[1:3]:
+        first_tile, last_tile = PAGE_ORDER[0], PAGE_ORDER[-1]
+        s_sb[first_tile] = new(f"s_sb{first_tile}", [P, V], F32)
+        nc.scalar.activation(s_sb[first_tile][:], s_ps[first_tile][:], ACT.Copy, scale=0.0625)
+        for t in PAGE_ORDER[1:-1]:
             scale_down(t)
 
-        grouped = new("grouped", [P, U, 4], BF16)
-        words = new("words", [P, U], I32)
-        scales = new("scales", [P, U], U8)
+        out_rows = out_0.rearrange("(p t) u -> p t u", t=PACK)
+        page_woven = new("page_woven", [P, U, PACK], BF16)
+        page_wd = new("page_wd", [P, U], I32)
+        page_sc = new("page_sc", [P, U], U8)
         half = U // 2
-        for t in order:
+        for t in PAGE_ORDER:
             nc.scalar.activation(page[t][:].indirect(n4_l[:]), s_sb[t][:], ACT.Copy)
             nc.sync.dma_start(out_rows[:, t, :], page[t][:])
-            if t != 1:
-                nc.vector.tensor_copy(grouped[:, :, t], page[t][:])
-            if t == 0:
-                scale_down(1, "s_sb0")
+            if t != last_tile:
+                nc.vector.tensor_copy(page_woven[:, :, t], page[t][:])
+            if t == first_tile:
+                scale_down(last_tile, f"s_sb{first_tile}")
+        nc.vector.tensor_copy(page_woven[:, :half, last_tile], page[last_tile][:, :half])
+        nc.vector.tensor_copy(page_woven[:, half:VECTOR_COLUMNS, last_tile], page[last_tile][:, half:VECTOR_COLUMNS])
+        nc.scalar.copy(page_woven[:, VECTOR_COLUMNS:, last_tile], page[last_tile][:, VECTOR_COLUMNS:])
+
         out_words = as_words(out_1)
-        nc.vector.tensor_copy(grouped[:, :half, 1], page[1][:, :half])
-        nc.vector.tensor_copy(grouped[:, half:576, 1], page[1][:, half:576])
-        nc.scalar.copy(grouped[:, 576:, 1], page[1][:, 576:])
         for h in range(2):
             cols = slice(half * h, half * (h + 1))
-            nc.vector.quantize_mx(out=words[:, cols].bitcast(FP8X4), scales=scales[:, cols], in_=grouped[:, cols, :].rearrange("p c t -> p (c t)"))
-            nc.sync.dma_start(out_words[:, cols], words[:, cols])
+            quantize(page_wd[:, cols], page_sc[:, cols], page_woven[:, cols, :])
+            nc.sync.dma_start(out_words[:, cols], page_wd[:, cols])
         for q in range(4):
             queue = nc.scalar if q % 2 else nc.sync
-            queue.dma_start(out_2[0, 4 * q : 4 * q + 4, :].bitcast(I32), scales[32 * q : 32 * q + 4, :].bitcast(I32))
+            queue.dma_start(out_2[0, 4 * q : 4 * q + 4, :].bitcast(I32), page_sc[32 * q : 32 * q + 4, :].bitcast(I32))

from contextlib import ExitStack

import concourse.mybir as mybir

F32 = mybir.dt.float32
BF16 = mybir.dt.bfloat16
I32 = mybir.dt.int32
U32 = mybir.dt.uint32
U16 = mybir.dt.uint16
U8 = mybir.dt.uint8
FP8X4 = mybir.dt.float8_e4m3fn_x4
ALU = mybir.AluOpType
ACT = mybir.ActivationFunctionType

P = 128
PACK = 4
LIST_ROWS = 16
K, T, S, V, H, U = 512, 2048, 512, 256, 512, 1024
FLOPS = 2 * K * H * S + 2 * K * H * V + 2 * H * S * V

PIECES = [(0, 0, S), (1, 0, S), (2, 0, S), (3, 0, S // 2), (3, S // 2, S)]

PAGE_ORDER = (0, 2, 3, 1)

VECTOR_COLUMNS = 576


def as_words(packed):
    return packed[0].rearrange("p n t -> p (n t)").bitcast(I32)


def block(dealt, t):
    return dealt[:, P * t : P * (t + 1)]


def tile_picked_kqghardrangepage_none_po_kernel(tc, x_words, x_scales, w1_words, w1_scales, w2_words, w2_scales, ga, gb, mem, offs, two, n1, n2, n3, n4, out_0, out_1, out_2):
    nc = tc.nc
    with ExitStack() as ctx:
        sb = ctx.enter_context(tc.tile_pool(name="sb", bufs=1))
        ps = ctx.enter_context(tc.psum_pool(name="ps", bufs=1))

        def new(name, shape, dtype, slot=None):
            return sb.tile(shape, dtype, name=name, tag=slot or name, align_bytes=64)

        def load_list(name, src):
            offsets = sb.tile(list(src.shape), U16, name=name)
            nc.sync.dma_start(offsets[:], src)
            return offsets

        def load_scales(dst, src):
            for q in range(4):
                nc.sync.dma_start(dst[32 * q : 32 * q + 4, :].bitcast(I32), src[0, 4 * q : 4 * q + 4, :].bitcast(I32))

        def product(out, lhs_words, lhs_scales, rhs_words, rhs_scales):
            nc.tensor.matmul_mx(out=out, lhsT=lhs_words.bitcast(FP8X4), lhsT_scale=lhs_scales, rhs=rhs_words[:].bitcast(FP8X4), rhs_scale=rhs_scales[:], start=True, stop=True)

        def quantize(words_out, scales_out, woven):
            nc.vector.quantize_mx(out=words_out.bitcast(FP8X4), scales=scales_out, in_=woven.rearrange("p c t -> p (c t)"))

        x_sc = new("x_sc", [P, T], U8, "page0")
        w2_sc_raw = new("w2_sc_raw", [P, H], U8, "xa")
        w1_sc_raw = new("w1_sc_raw", [P, H], U8, "ends")
        nc.vector.memset(x_sc[:, : T // 2].bitcast(I32), 0)
        nc.gpsimd.memset(x_sc[:, T // 2 :].bitcast(I32), 0)
        for raw in (w2_sc_raw, w1_sc_raw):
            nc.gpsimd.memset(raw[:].bitcast(I32), 0)

        two_l = load_list("two_l", two)
        offs_l = load_list("offs_l", offs)
        w2_raw = new("w2_raw", [P, H], I32, "page1")
        nc.sync.dma_start(w2_raw[:], as_words(w2_words))
        load_scales(x_sc, x_scales)
        x_wd = new("x_wd", [P, T], I32, "page2")
        nc.sync.dma_start(x_wd[:], as_words(x_words))
        load_scales(w2_sc_raw, w2_scales)
        n2_l = load_list("n2_l", n2)
        n3_l = load_list("n3_l", n3)
        w1_raw = new("w1_raw", [P, H], I32)
        nc.sync.dma_start(w1_raw[:], as_words(w1_words))
        load_scales(w1_sc_raw, w1_scales)
        n1_l = load_list("n1_l", n1)

        b_win = [new(f"b_win{t}", [P, 2 * V], F32) for t in range(PACK)]
        a_win = [new(f"a_win{t}", [P, (2 * S if t < PACK - 1 else S) + LIST_ROWS], F32) for t in range(PACK)]
        for t in range(PACK):
            nc.vector.memset(b_win[t][:, V:], 0.0)
        warm = new("warm", [P, 1], F32)
        nc.scalar.activation(warm[:], b_win[0][:, V : V + 1], ACT.Sigmoid)
        for t in range(PACK):
            nc.vector.memset(a_win[t][:, S:], 0.0)

        gb_t = new("gb_t", [P, PACK], F32)
        nc.sync.dma_start(gb_t[:], gb.rearrange("(p t) o -> p (t o)", t=PACK))
        ga_t = new("ga_t", [P, PACK], F32)
        nc.sync.dma_start(ga_t[:], ga.rearrange("(p t) o -> p (t o)", t=PACK))
        n4_l = load_list("n4_l", n4)

        def deal_scales(dst, src):
            nc.vector.tensor_copy(dst[:].rearrange("p (t m) -> p t m", t=PACK), src[:].rearrange("p (m t) -> p t m", t=PACK))

        w2 = new("w2", [P, H], I32, "page3")
        nc.vector.tensor_copy(w2[:].rearrange("p (t m) -> p m t", t=PACK), w2_raw[:].rearrange("p (m t) -> p m t", t=PACK))
        xb_sc = new("xb_sc", [P, V], U8, "w1_second")
        nc.vector.tensor_copy(xb_sc[:], x_sc[:].indirect(two_l[:]))
        xa_sc = new("xa_sc", [P, S], U8)
        nc.vector.tensor_copy(xa_sc[:], x_sc[:].indirect(offs_l[:]))
        xb = new("xb", [P, V], U32, "w1_sc")
        nc.vector.tensor_copy(xb[:], x_wd[:].bitcast(U32).indirect(two_l[:]))
        w2_sc = new("w2_sc", [P, H], U8)
        deal_scales(w2_sc, w2_sc_raw)

        b_ps = [ps.tile([P, 2, V], F32, name=f"b_ps{h}") for h in range(2)]
        for t in range(PACK):
            product(b_ps[t // 2][:, t % 2, :], block(w2, t), block(w2_sc, t), xb, xb_sc)

        xa = new("xa", [P, S], U32)
        nc.vector.tensor_copy(xa[:], x_wd[:].bitcast(U32).indirect(offs_l[:]))
        for t in (2, 3):
            nc.vector.tensor_copy(b_win[t][:, :V], b_ps[1][:, t % 2, :])
        w1_sc = new("w1_sc", [P, H], U8)
        deal_scales(w1_sc, w1_sc_raw)
        w1 = [new("w1_first", [P, H // 2], I32, "ends"), new("w1_second", [P, H // 2], I32)]
        for h in range(2):
            nc.vector.tensor_copy(w1[h][:].rearrange("p (t m) -> p m t", t=2), w1_raw[:].rearrange("p (m t) -> p m t", t=PACK)[:, :, 2 * h : 2 * h + 2])
        a_ps = [ps.tile([P, S], F32, name=f"a_ps{t}") for t in range(2)]
        for t in range(2):
            product(a_ps[t][:], block(w1[0], t), block(w1_sc, t), xa, xa_sc)

        mem_rows = mem.rearrange("(p t) u -> p t u", t=PACK)
        page = [new(f"page{t}", [P, U], F32) for t in range(PACK)]
        for t in range(PACK):
            nc.sync.dma_start(page[t][:], mem_rows[:, t, :])

        pa = [new(f"pa{h}", [P, 2, V], F32) for h in range(2)]
        pb = [new(f"pb{h}", [P, 2, V], F32) for h in range(2)]
        for t in range(PACK):
            if t < 2:
                nc.scalar.copy(b_win[t][:, :V], b_ps[0][:, t, :])
            nc.scalar.activation(pa[t // 2][:, t % 2, :], b_win[t][:].indirect(n2_l[:]), ACT.Copy)
            nc.scalar.activation(pb[t // 2][:, t % 2, :], b_win[t][:].indirect(n3_l[:]), ACT.Copy)
        for t in range(2):
            nc.vector.tensor_copy(a_win[t][:, :S], a_ps[t][:])

        spread = new("spread", [P, PACK, V], F32)
        top, low = {}, {}

        def ends_of_three(h):
            ends = new(f"ends{h}", [P, 2, 2, V], F32, "ends")
            nc.vector.tensor_tensor(ends[:, 0], pa[h][:], pb[h][:], ALU.min)
            nc.vector.tensor_tensor(ends[:, 1], pa[h][:], pb[h][:], ALU.max)
            low[h] = new(f"low{h}", [P, 2, V], F32, "mn" if h else None)
            top[h] = new(f"top{h}", [P, 2, V], F32)
            nc.vector.tensor_tensor(low[h][:], ends[:, 0], b_ps[h][:], ALU.min)
            nc.vector.tensor_tensor(top[h][:], ends[:, 1], b_ps[h][:], ALU.max)
            a_ps.append(ps.tile([P, S], F32, name=f"a_ps{2 + h}", tag=f"b_ps{h}"))
            product(a_ps[2 + h][:], block(w1[1], h), block(w1_sc, 2 + h), xa, xa_sc)

        def spread_of(h):
            nc.vector.scalar_tensor_tensor(spread[:, 2 * h : 2 * h + 2, :], low[h][:], -0.5, top[h][:], ALU.mult, ALU.add)

        mb, mx, mn, sg, diff = {}, {}, {}, {}, {}
        z_bf = new("z_bf", [P, PACK, S], BF16)
        z_woven = new("z_woven", [P, S, PACK], BF16)
        z2_woven = new("z2_woven", [P, V, PACK], BF16)
        z2_wd = new("z2_wd", [P, V], U32)
        z2_sc = new("z2_sc", [P, V], U8)

        mx_slot = ["ends", "spread", "diff0", "diff1", "diff2"]

        def fetch(i):
            t, first, end = PIECES[i]
            if t >= 2 and first == 0:
                nc.scalar.copy(a_win[t][:, :S], a_ps[t][:])
            mb[i] = new(f"mb{i}", [P, 2 * (end - first)], F32, mx_slot[i - 2] if i >= 2 else None)
            nc.scalar.activation(mb[i][:], a_win[t][:].indirect(n1_l[:, 2 * first // LIST_ROWS : 2 * end // LIST_ROWS]), ACT.Copy)

        def larger(i):
            t, first, end = PIECES[i]
            members = mb[i][:].rearrange("p (j e) -> p j e", e=2)
            mx[i] = new(f"mx{i}", [P, end - first], F32, mx_slot[i])
            nc.vector.tensor_tensor(mx[i][:], members[:, :, 0], members[:, :, 1], ALU.max)
            sg[i] = new(f"sg{i}", [P, end - first], F32)
            nc.scalar.activation(sg[i][:], mx[i][:], ACT.Sigmoid)

        def smaller(i):
            t, first, end = PIECES[i]
            members = mb[i][:].rearrange("p (j e) -> p j e", e=2)
            mn[i] = new(f"mn{i}", [P, end - first], F32, "mn")
            nc.vector.tensor_tensor(mn[i][:], members[:, :, 0], members[:, :, 1], ALU.min)

        def differ(i):
            t, first, end = PIECES[i]
            diff[i] = new(f"diff{i}", [P, end - first], F32)
            nc.vector.tensor_tensor(diff[i][:], a_win[t][:, first:end], mn[i][:], ALU.subtract)

        def gate(i):
            t, first, end = PIECES[i]
            nc.vector.scalar_tensor_tensor(
                z_bf[:, t, :].rearrange("p (s m) -> p m s", s=PACK)[:, first // PACK : end // PACK, :],
                diff[i][:].rearrange("p (m s) -> p m s", s=PACK),
                ga_t[:, t : t + 1],
                sg[i][:].rearrange("p (m s) -> p m s", s=PACK),
                ALU.mult,
                ALU.mult,
            )

        def weave_z(copy, h, blocks):
            copy(
                z_woven[:].rearrange("p (s h c i) t -> p h s c t i", s=PACK, h=2, i=4)[:, h, blocks],
                z_bf[:].rearrange("p t (s h c i) -> p h s c t i", s=PACK, h=2, i=4)[:, h, blocks],
            )

        ends_of_three(0)
        spread_of(0)
        ends_of_three(1)
        fetch(0)
        fetch(1)
        larger(0)
        spread_of(1)
        smaller(0)
        nc.vector.tensor_tensor(
            z2_woven[:].rearrange("p (c i) t -> p c t i", i=4),
            spread[:].rearrange("p t (c i) -> p c t i", i=4),
            gb_t[:].unsqueeze(1).unsqueeze(3).broadcast_to([P, V // 4, PACK, 4]),
            ALU.mult,
        )
        differ(0)
        fetch(2)
        larger(1)
        quantize(z2_wd[:], z2_sc[:], z2_woven[:])
        smaller(1)
        gate(0)
        for i in (2, 3):
            fetch(i + 1)
            larger(i)
            differ(i - 1)
            smaller(i)
            gate(i - 1)
        differ(3)
        larger(4)
        smaller(4)
        gate(3)
        weave_z(nc.scalar.copy, 0, slice(0, 1))
        weave_z(nc.scalar.copy, 0, slice(1, PACK))
        differ(4)
        gate(4)
        z_wd = new("z_wd", [P, S], U32)
        z_sc = new("z_sc", [P, S], U8)
        for step in range(PACK + 1):
            if step < PACK:
                weave_z(nc.vector.tensor_copy, 1, slice(PAGE_ORDER[step], PAGE_ORDER[step] + 1))
            if step > 0:
                t = PAGE_ORDER[step - 1]
                quantize(block(z_wd, t), block(z_sc, t), z_woven[:, P * t : P * (t + 1), :])

        s_ps = {t: ps.tile([P, V], F32, name=f"s_ps{t}") for t in PAGE_ORDER}
        s_sb = {}
        for t in PAGE_ORDER:
            product(s_ps[t][:], block(z_wd, t), block(z_sc, t), z2_wd, z2_sc)

        def scale_down(t, slot=None):
            s_sb[t] = new(f"s_sb{t}", [P, V], F32, slot)
            nc.vector.tensor_scalar(s_sb[t][:], s_ps[t][:], 0.0625, None, ALU.mult)

        first_tile, last_tile = PAGE_ORDER[0], PAGE_ORDER[-1]
        s_sb[first_tile] = new(f"s_sb{first_tile}", [P, V], F32)
        nc.scalar.activation(s_sb[first_tile][:], s_ps[first_tile][:], ACT.Copy, scale=0.0625)
        for t in PAGE_ORDER[1:-1]:
            scale_down(t)

        out_rows = out_0.rearrange("(p t) u -> p t u", t=PACK)
        page_woven = new("page_woven", [P, U, PACK], BF16)
        page_wd = new("page_wd", [P, U], I32)
        page_sc = new("page_sc", [P, U], U8)
        half = U // 2
        for t in PAGE_ORDER:
            nc.scalar.activation(page[t][:].indirect(n4_l[:]), s_sb[t][:], ACT.Copy)
            nc.sync.dma_start(out_rows[:, t, :], page[t][:])
            if t != last_tile:
                nc.vector.tensor_copy(page_woven[:, :, t], page[t][:])
            if t == first_tile:
                scale_down(last_tile, f"s_sb{first_tile}")
        nc.vector.tensor_copy(page_woven[:, :half, last_tile], page[last_tile][:, :half])
        nc.vector.tensor_copy(page_woven[:, half:VECTOR_COLUMNS, last_tile], page[last_tile][:, half:VECTOR_COLUMNS])
        nc.scalar.copy(page_woven[:, VECTOR_COLUMNS:, last_tile], page[last_tile][:, VECTOR_COLUMNS:])

        out_words = as_words(out_1)
        for h in range(2):
            cols = slice(half * h, half * (h + 1))
            quantize(page_wd[:, cols], page_sc[:, cols], page_woven[:, cols, :])
            nc.sync.dma_start(out_words[:, cols], page_wd[:, cols])
        for q in range(4):
            queue = nc.scalar if q % 2 else nc.sync
            queue.dma_start(out_2[0, 4 * q : 4 * q + 4, :].bitcast(I32), page_sc[32 * q : 32 * q + 4, :].bitcast(I32))
